import numpy as np
import ml_dtypes


def mxq(x, axis, fmt="e4m3"):
    dtype, down = {"e4m3": (ml_dtypes.float8_e4m3fn, 7), "e5m2": (ml_dtypes.float8_e5m2, 14)}[fmt]
    v = np.moveaxis(np.asarray(x, np.float32).astype(ml_dtypes.bfloat16).astype(np.float64), axis, -1)
    blocks = v.reshape(v.shape[:-1] + (-1, 32))
    amax = np.abs(blocks).max(-1, keepdims=True)
    byte = np.maximum(np.where(amax > 0, np.frexp(amax)[1] - 1 + 127, 0) - down, 1)
    scale = np.exp2(byte - 127.0)
    codes = (blocks / scale).astype(np.float32).astype(dtype).astype(np.float64)
    return np.moveaxis((codes * scale).reshape(v.shape), -1, axis)


WIDE = False


def mx_kscale(k):
    if not WIDE:
        return np.ones(k)
    levels = np.array([10, -10, 5, -5, 0])
    if k % 512:
        return np.exp2(np.random.permutation(np.resize(levels, k // 32))).repeat(32)
    a = np.empty((k // 512, 16))
    for p in range(k // 512):
        a[p, :8] = np.random.permutation(np.resize(levels, 8))
        for g in range(8):
            far = levels[np.abs(levels - a[p, g]) >= 10]
            a[p, g + 8] = far[np.random.randint(len(far))]
    return np.exp2(a.ravel()).repeat(32)


def f64(x):
    return np.asarray(x).astype(np.float64)


def striped(idx):
    return np.tile(idx.reshape(-1, 16).T, (8, 1)).astype(np.uint16)


def unstriped(offs):
    return offs[:16].T.reshape(-1).astype(np.int64)


def pack_weight(w):
    k, n = w.shape
    w = f64(np.asarray(w, np.float32).astype(ml_dtypes.bfloat16)).reshape(k // 32, 32, n)
    amax = np.abs(w).max(1)
    byte = np.clip(np.where(amax > 0, np.frexp(amax)[1] - 1 + 127 - 7, 1), 1, 254)
    scaled = (w * np.exp2(127.0 - byte)[:, None, :]).reshape(k, n).astype(np.float32)
    words = np.ascontiguousarray(scaled.reshape(k // 512, 128, 4, n).transpose(0, 1, 3, 2)).astype(ml_dtypes.float8_e4m3fn).view(np.uint8)
    return words, np.ascontiguousarray(byte.astype(np.uint8).reshape(k // 512, 16, n))


def unpack_weight(words, scales):
    g, p, n, _ = words.shape
    vals = np.ascontiguousarray(words).view(ml_dtypes.float8_e4m3fn).astype(np.float64) * np.repeat(np.exp2(scales.astype(np.float64) - 127.0), 8, axis=1)[..., None]
    return vals.transpose(0, 1, 3, 2).reshape(g * 512, n)


K, T, S, N, U = 512, 1024, 512, 128, 512
P = 2 ** 7


def setup_inputs():
    n = np.random.standard_normal
    s = mx_kscale(K)[:, None]
    packed_xT = pack_weight(n((K, T)) * s)
    return {
        "x_words": packed_xT[0],
        "x_scales": packed_xT[1],
        "w1": (n((K, N)) / np.sqrt(K) / s).astype(np.float32),
        "im": (np.tile(np.random.uniform(0.2, 1.5, S), (P, 1))).astype(np.float32),
        "lam": (np.tile(n(U) * 0.3, (P, 1))).astype(np.float32),
        "comp": (np.tile(np.random.uniform(0.05, 0.6, U), (P, 1))).astype(np.float32),
        "rest": (np.tile(np.random.uniform(0.3, 1.2, U), (P, 1))).astype(np.float32),
        "offs": striped(np.random.permutation(T)[:S]),
        "pa": striped(np.random.randint(0, S, U)),
        "pb": striped(np.random.randint(0, S, U)),
    }


def reference(x_words, x_scales, w1, im, lam, comp, rest, offs, pa, pb):
    xq = unpack_weight(x_words, x_scales)[:, unstriped(offs)]
    y = mxq(f64(w1), 0, "e4m3").T @ xq
    df = y[:, unstriped(pa)] - y[:, unstriped(pb)]
    ln = np.sqrt((df) ** 2 + 0.02)
    cons = ln - f64(rest)[:1]
    dl = (-1.0 * (cons + f64(comp)[:1] * f64(lam)[:1])) / (f64(im)[:1][:, unstriped(pa)] + f64(im)[:1][:, unstriped(pb)] + f64(comp)[:1])
    return f64(lam)[:1] + dl

@@ -1,0 +1,190 @@
+from contextlib import ExitStack
+
+import concourse.mybir as mybir
+from concourse.masks import make_identity
+
+K, T, S, N, U = 512, 1024, 512, 128, 512
+FLOPS = 2 * K * N * S
+
+F32 = mybir.dt.float32
+BF16 = mybir.dt.bfloat16
+I32 = mybir.dt.int32
+U32 = mybir.dt.uint32
+U16 = mybir.dt.uint16
+U8 = mybir.dt.uint8
+FP8X4 = mybir.dt.float8_e4m3fn_x4
+ALU = mybir.AluOpType
+ACT = mybir.ActivationFunctionType
+
+P = 128
+PACK = 4
+LIST_ROWS = 16
+HALF = U // 2
+BLOCK = 128
+SOFT = 0.02
+PICK_CHUNKS = ((0, 256), (256, 128), (384, 128))
+
+
+def entries(offsets, first, count):
+    return offsets[:, first // LIST_ROWS : (first + count) // LIST_ROWS]
+
+
+def tile_picked_yxpbd_lam_p_kernel(
+    tc, x_words, x_scales, w1, im, lam, comp, rest, offs, pa, pb, out
+):
+    nc = tc.nc
+    with ExitStack() as ctx:
+        lists = ctx.enter_context(tc.tile_pool(name="lists", bufs=1))
+        sb = ctx.enter_context(tc.tile_pool(name="sb", bufs=1))
+        psum = ctx.enter_context(tc.psum_pool(name="psum", bufs=1))
+
+        offs_t = lists.tile([P, S // LIST_ROWS], U16, name="offs_t")
+        pa_t = lists.tile([P, U // LIST_ROWS], U16, name="pa_t")
+        pb_t = lists.tile([P, U // LIST_ROWS], U16, name="pb_t")
+
+        scale_table = sb.tile([P, T], U8, name="scale_table", align_bytes=64)
+        word_table = sb.tile([P, T], U32, name="word_table", align_bytes=64)
+        im_table = sb.tile([P, S], F32, name="im_table", align_bytes=64)
+        w_raw = sb.tile([P, PACK, N], F32, name="w_raw", align_bytes=64)
+        rows = sb.tile([P, BLOCK], F32, name="rows", align_bytes=64)
+        ident = sb.tile([P, P], F32, name="ident", align_bytes=64)
+        one = sb.tile([P, 1], F32, name="one")
+        warm = sb.tile([P, 1], F32, name="warm")
+
+        nc.vector.memset(scale_table[:].bitcast(I32), 0)
+        nc.sync.dma_start(pa_t[:], pa)
+        nc.sync.dma_start(im_table[0:32, :], im[0:32, :])
+        nc.sync.dma_start(offs_t[:], offs)
+        nc.sync.dma_start(w_raw[:], w1.rearrange("(p j) m -> p j m", j=PACK))
+        nc.sync.dma_start(
+            word_table[:].bitcast(I32), x_words[0].rearrange("p n t -> p (n t)").bitcast(I32)
+        )
+        for q in range(4):
+            nc.sync.dma_start(
+                scale_table[32 * q : 32 * q + 4, :].bitcast(I32),
+                x_scales[0, 4 * q : 4 * q + 4, :].bitcast(I32),
+            )
+        nc.sync.dma_start(pb_t[:], pb)
+        nc.vector.memset(im_table[32:64, :], 0.0)
+        nc.vector.memset(im_table[64:128, :], 0.0)
+        nc.gpsimd.memset(one[:], 1.0)
+        nc.scalar.activation(warm[:], one[:], ACT.Sqrt)
+        nc.gpsimd.memset(rows[:], 0.0)
+        make_identity(nc, ident[:])
+        for g, src in enumerate((lam, comp, rest)):
+            blocks = src.rearrange("a (t c) -> (a t) c", c=BLOCK)
+            nc.sync.dma_start(rows[32 * g : 32 * g + 4, :], blocks[0:4, :])
+
+        im_a = [sb.tile([P, HALF], F32, name=f"im_a{h}", align_bytes=64) for h in range(2)]
+        for h in range(2):
+            nc.vector.tensor_copy(im_a[h][:], im_table[:].indirect(entries(pa_t, h * HALF, HALF)))
+
+        w_grouped = sb.tile([P, N, PACK], BF16, name="w_grouped", tag="staged", align_bytes=64)
+        w_codes = sb.tile([P, N], U32, name="w_codes", align_bytes=64)
+        w_scales = sb.tile([P, N], U8, name="w_scales", align_bytes=64)
+        nc.scalar.copy(w_grouped[:], w_raw[:].rearrange("p j m -> p m j"))
+        nc.vector.quantize_mx(
+            out=w_codes[:].bitcast(FP8X4),
+            scales=w_scales[:],
+            in_=w_grouped[:].rearrange("p m j -> p (m j)"),
+        )
+
+        words = sb.tile([P, S], U32, name="words", align_bytes=64)
+        nc.vector.tensor_copy(words[:], word_table[:].indirect(offs_t[:]))
+
+        y = sb.tile([P, S], F32, name="y", align_bytes=64)
+        for c, (first, count) in enumerate(PICK_CHUNKS):
+            scales = sb.tile([P, count], U8, name=f"scales{c}", align_bytes=64)
+            nc.vector.tensor_copy(scales[:], scale_table[:].indirect(entries(offs_t, first, count)))
+            acc = psum.tile([P, count], F32, name=f"acc{c}")
+            nc.tensor.matmul_mx(
+                out=acc[:],
+                lhsT=w_codes[:].bitcast(FP8X4),
+                lhsT_scale=w_scales[:],
+                rhs=words[:, first : first + count].bitcast(FP8X4),
+                rhs_scale=scales[:],
+                start=True,
+                stop=True,
+            )
+            nc.scalar.copy(y[:, first : first + count], acc[:])
+
+        cols = sb.tile([P, 3, PACK], F32, name="cols")
+        rows_t = psum.tile([P, 4, 32], F32, name="rows_t")
+        nc.tensor.transpose(rows_t[:].rearrange("p g c -> p (g c)"), rows[:], ident[:])
+        nc.scalar.copy(cols[:], rows_t[:, 0:3, 0:PACK])
+
+        diff = sb.tile([P, U], F32, name="diff", align_bytes=64)
+        den = diff[:, 0:U:BLOCK]
+        inv = sb.tile([P, 4], F32, name="inv")
+        top = sb.tile([P, 4], F32, name="top")
+        im_sum = sb.tile([P, U], F32, name="im_sum", tag="staged", align_bytes=64)
+        for h in range(2):
+            nc.vector.tensor_tensor(
+                im_sum[:, h * HALF : (h + 1) * HALF],
+                im_table[:].indirect(entries(pb_t, h * HALF, HALF)),
+                im_a[h][:],
+                ALU.add,
+            )
+            sum_t = psum.tile([P, 2, BLOCK], F32, name=f"sum_t{h}")
+            for b in range(2):
+                t = 2 * h + b
+                nc.tensor.transpose(sum_t[:, b, :], im_sum[:, t * BLOCK : (t + 1) * BLOCK], ident[:])
+            for b in range(2):
+                t = 2 * h + b
+                nc.scalar.activation(
+                    den[:, t : t + 1], sum_t[:, b, 0:1], ACT.Identity, bias=cols[:, 1, t : t + 1]
+                )
+            for b in range(2):
+                t = 2 * h + b
+                nc.scalar.activation(
+                    top[:, t : t + 1],
+                    sum_t[:, b, 0:1],
+                    ACT.Identity,
+                    bias=cols[:, 2, t : t + 1],
+                    scale=cols[:, 0, t : t + 1],
+                )
+
+        y_a = [sb.tile([P, HALF], F32, name=f"y_a{h}", align_bytes=64) for h in range(2)]
+        for h in range(2):
+            nc.vector.tensor_copy(y_a[h][:], y[:].indirect(entries(pa_t, h * HALF, HALF)))
+        nc.vector.reciprocal(inv[:], den)
+        spread = []
+        for name, col in (("top_rows", top), ("inv_rows", inv)):
+            bank = psum.tile([P, U], F32, name=name)
+            for t in range(4):
+                nc.tensor.transpose(
+                    bank[:, t * BLOCK : (t + 1) * BLOCK], col[:, t : t + 1].to_broadcast([P, P]), ident[:]
+                )
+            spread.append(bank)
+        top_rows, inv_rows = spread
+
+        length = []
+        for t in range(4):
+            h, b = divmod(t, 2)
+            cs = slice(t * BLOCK, (t + 1) * BLOCK)
+            nc.vector.tensor_tensor(
+                diff[:, cs],
+                y[:].indirect(entries(pb_t, t * BLOCK, BLOCK)),
+                y_a[h][:, b * BLOCK : (b + 1) * BLOCK],
+                ALU.subtract,
+            )
+            sq = sb.tile([P, BLOCK], F32, name=f"sq{t}", align_bytes=64)
+            ln = sb.tile([P, BLOCK], F32, name=f"ln{t}", align_bytes=64)
+            nc.scalar.activation(sq[:], diff[:, cs], ACT.Square)
+            nc.scalar.activation(ln[:], sq[:], ACT.Sqrt, bias=SOFT)
+            length.append(ln)
+        for h in range(2):
+            gap = sb.tile([P, HALF], F32, name=f"gap{h}", align_bytes=64)
+            res = sb.tile([P, HALF], F32, name=f"res{h}", align_bytes=64)
+            for b in range(2):
+                t = 2 * h + b
+                cs = slice(t * BLOCK, (t + 1) * BLOCK)
+                nc.vector.tensor_tensor(
+                    gap[:, b * BLOCK : (b + 1) * BLOCK], top_rows[:, cs], length[t][:], ALU.subtract
+                )
+            for b in range(2):
+                t = 2 * h + b
+                cs = slice(t * BLOCK, (t + 1) * BLOCK)
+                bs = slice(b * BLOCK, (b + 1) * BLOCK)
+                nc.vector.tensor_tensor(res[:, bs], gap[:, bs], inv_rows[:, cs], ALU.mult)
+            nc.sync.dma_start(out[:, h * HALF : (h + 1) * HALF], res[:])

@@ -22,6 +22,7 @@ LIST_ROWS = 16
 HALF = U // 2
 BLOCK = 128
 SOFT = 0.02
+SUM_CHUNKS = ((0, 2), (2, 1), (3, 1))
 PICK_CHUNKS = ((0, 256), (256, 128), (384, 128))
 
 
@@ -36,6 +37,7 @@ def tile_picked_yxpbd_lam_p_kernel(
     with ExitStack() as ctx:
         lists = ctx.enter_context(tc.tile_pool(name="lists", bufs=1))
         sb = ctx.enter_context(tc.tile_pool(name="sb", bufs=1))
+        shared = ctx.enter_context(tc.tile_pool(name="shared", bufs=1))
         psum = ctx.enter_context(tc.psum_pool(name="psum", bufs=1))
 
         offs_t = lists.tile([P, S // LIST_ROWS], U16, name="offs_t")
@@ -45,6 +47,7 @@ def tile_picked_yxpbd_lam_p_kernel(
         scale_table = sb.tile([P, T], U8, name="scale_table", align_bytes=64)
         word_table = sb.tile([P, T], U32, name="word_table", align_bytes=64)
         im_table = sb.tile([P, S], F32, name="im_table", align_bytes=64)
+        comp_rows = sb.tile([P, U], F32, name="comp_rows", align_bytes=64)
         w_raw = sb.tile([P, PACK, N], F32, name="w_raw", align_bytes=64)
         rows = sb.tile([P, BLOCK], F32, name="rows", align_bytes=64)
         ident = sb.tile([P, P], F32, name="ident", align_bytes=64)
@@ -53,33 +56,38 @@ def tile_picked_yxpbd_lam_p_kernel(
 
         nc.vector.memset(scale_table[:].bitcast(I32), 0)
         nc.sync.dma_start(pa_t[:], pa)
-        nc.sync.dma_start(im_table[0:32, :], im[0:32, :])
+        nc.sync.dma_start(im_table[0:64, :], im[0:64, :])
+        nc.sync.dma_start(comp_rows[0:32, :], comp[0:32, :])
         nc.sync.dma_start(offs_t[:], offs)
-        nc.sync.dma_start(w_raw[:], w1.rearrange("(p j) m -> p j m", j=PACK))
         nc.sync.dma_start(
             word_table[:].bitcast(I32), x_words[0].rearrange("p n t -> p (n t)").bitcast(I32)
         )
+        nc.sync.dma_start(w_raw[:], w1.rearrange("(p j) m -> p j m", j=PACK))
         for q in range(4):
             nc.sync.dma_start(
                 scale_table[32 * q : 32 * q + 4, :].bitcast(I32),
                 x_scales[0, 4 * q : 4 * q + 4, :].bitcast(I32),
             )
         nc.sync.dma_start(pb_t[:], pb)
-        nc.vector.memset(im_table[32:64, :], 0.0)
         nc.vector.memset(im_table[64:128, :], 0.0)
+        nc.vector.memset(comp_rows[32:64, :], 0.0)
+        nc.vector.memset(comp_rows[64:128, :], 0.0)
         nc.gpsimd.memset(one[:], 1.0)
         nc.scalar.activation(warm[:], one[:], ACT.Sqrt)
         nc.gpsimd.memset(rows[:], 0.0)
         make_identity(nc, ident[:])
-        for g, src in enumerate((lam, comp, rest)):
+        for g, src in enumerate((lam, rest)):
             blocks = src.rearrange("a (t c) -> (a t) c", c=BLOCK)
             nc.sync.dma_start(rows[32 * g : 32 * g + 4, :], blocks[0:4, :])
 
-        im_a = [sb.tile([P, HALF], F32, name=f"im_a{h}", align_bytes=64) for h in range(2)]
+        im_a = sb.tile([P, U], F32, name="im_a", align_bytes=64)
         for h in range(2):
-            nc.vector.tensor_copy(im_a[h][:], im_table[:].indirect(entries(pa_t, h * HALF, HALF)))
+            cs = slice(h * HALF, (h + 1) * HALF)
+            nc.vector.tensor_tensor(
+                im_a[:, cs], im_table[:].indirect(entries(pa_t, h * HALF, HALF)), comp_rows[:, cs], ALU.add
+            )
 
-        w_grouped = sb.tile([P, N, PACK], BF16, name="w_grouped", tag="staged", align_bytes=64)
+        w_grouped = shared.tile([P, N, PACK], BF16, name="w_grouped", align_bytes=64, offset=0)
         w_codes = sb.tile([P, N], U32, name="w_codes", align_bytes=64)
         w_scales = sb.tile([P, N], U8, name="w_scales", align_bytes=64)
         nc.scalar.copy(w_grouped[:], w_raw[:].rearrange("p j m -> p m j"))
@@ -94,7 +102,10 @@ def tile_picked_yxpbd_lam_p_kernel(
 
         y = sb.tile([P, S], F32, name="y", align_bytes=64)
         for c, (first, count) in enumerate(PICK_CHUNKS):
-            scales = sb.tile([P, count], U8, name=f"scales{c}", align_bytes=64)
+            if c == 0:
+                scales = sb.tile([P, count], U8, name="scales0", align_bytes=64)
+            else:
+                scales = shared.tile([P, count], U8, name=f"scales{c}", align_bytes=64, offset=first - HALF)
             nc.vector.tensor_copy(scales[:], scale_table[:].indirect(entries(offs_t, first, count)))
             acc = psum.tile([P, count], F32, name=f"acc{c}")
             nc.tensor.matmul_mx(
@@ -108,83 +119,78 @@ def tile_picked_yxpbd_lam_p_kernel(
             )
             nc.scalar.copy(y[:, first : first + count], acc[:])
 
-        cols = sb.tile([P, 3, PACK], F32, name="cols")
+        work = sb.tile([P, 8, BLOCK], F32, name="work", align_bytes=64)
+        diff = work[:, 0:4, :]
+        sq = work[:, 4:8, :]
+        cols = work[:, 2:6, 0:2]
         rows_t = psum.tile([P, 4, 32], F32, name="rows_t")
         nc.tensor.transpose(rows_t[:].rearrange("p g c -> p (g c)"), rows[:], ident[:])
-        nc.scalar.copy(cols[:], rows_t[:, 0:3, 0:PACK])
+        nc.scalar.copy(cols, rows_t[:, 0:2, 0:4].rearrange("p g t -> p t g"))
 
-        diff = sb.tile([P, U], F32, name="diff", align_bytes=64)
-        den = diff[:, 0:U:BLOCK]
-        inv = sb.tile([P, 4], F32, name="inv")
-        top = sb.tile([P, 4], F32, name="top")
-        im_sum = sb.tile([P, U], F32, name="im_sum", tag="staged", align_bytes=64)
-        for h in range(2):
+        im_sum = shared.tile([P, U], F32, name="im_sum", align_bytes=64, offset=HALF)
+        sum_t = psum.tile([P, 4, 4, 32], F32, name="sum_t")
+        for first, blocks in SUM_CHUNKS:
+            cs = slice(first * BLOCK, (first + blocks) * BLOCK)
             nc.vector.tensor_tensor(
-                im_sum[:, h * HALF : (h + 1) * HALF],
-                im_table[:].indirect(entries(pb_t, h * HALF, HALF)),
-                im_a[h][:],
+                im_sum[:, cs],
+                im_table[:].indirect(entries(pb_t, cs.start, blocks * BLOCK)),
+                im_a[:, cs],
                 ALU.add,
             )
-            sum_t = psum.tile([P, 2, BLOCK], F32, name=f"sum_t{h}")
-            for b in range(2):
-                t = 2 * h + b
-                nc.tensor.transpose(sum_t[:, b, :], im_sum[:, t * BLOCK : (t + 1) * BLOCK], ident[:])
-            for b in range(2):
-                t = 2 * h + b
-                nc.scalar.activation(
-                    den[:, t : t + 1], sum_t[:, b, 0:1], ACT.Identity, bias=cols[:, 1, t : t + 1]
-                )
-            for b in range(2):
-                t = 2 * h + b
-                nc.scalar.activation(
-                    top[:, t : t + 1],
-                    sum_t[:, b, 0:1],
-                    ACT.Identity,
-                    bias=cols[:, 2, t : t + 1],
-                    scale=cols[:, 0, t : t + 1],
-                )
-
-        y_a = [sb.tile([P, HALF], F32, name=f"y_a{h}", align_bytes=64) for h in range(2)]
-        for h in range(2):
-            nc.vector.tensor_copy(y_a[h][:], y[:].indirect(entries(pa_t, h * HALF, HALF)))
-        nc.vector.reciprocal(inv[:], den)
-        spread = []
-        for name, col in (("top_rows", top), ("inv_rows", inv)):
-            bank = psum.tile([P, U], F32, name=name)
-            for t in range(4):
+            for t in range(first, first + blocks):
                 nc.tensor.transpose(
-                    bank[:, t * BLOCK : (t + 1) * BLOCK], col[:, t : t + 1].to_broadcast([P, P]), ident[:]
+                    sum_t[:, t].rearrange("p q c -> p (q c)"), im_sum[:, t * BLOCK : (t + 1) * BLOCK], ident[:]
                 )
-            spread.append(bank)
-        top_rows, inv_rows = spread
-
-        length = []
+        sums = sb.tile([P, 2, 4], F32, name="sums")
+        nc.scalar.copy(sums[:], sum_t[:, :, 0:2, 0].rearrange("p t q -> p q t"))
+        top = sb.tile([P, 4], F32, name="top")
         for t in range(4):
-            h, b = divmod(t, 2)
-            cs = slice(t * BLOCK, (t + 1) * BLOCK)
+            nc.scalar.activation(
+                top[:, t : t + 1],
+                sums[:, 1, t : t + 1],
+                ACT.Identity,
+                bias=cols[:, t, 1:2],
+                scale=cols[:, t, 0:1],
+            )
+
+        y_a = sb.tile([P, U], F32, name="y_a", align_bytes=64)
+        for h in range(2):
+            nc.vector.tensor_copy(
+                y_a[:, h * HALF : (h + 1) * HALF], y[:].indirect(entries(pa_t, h * HALF, HALF))
+            )
+        inv = sb.tile([P, 4], F32, name="inv")
+        nc.vector.reciprocal(inv[:], sums[:, 0, :])
+        spread = []
+        for h in range(2):
+            bank = psum.tile([P, 2, 2, BLOCK], F32, name=f"spread{h}")
+            for kind, col in enumerate((top, inv)):
+                for b in range(2):
+                    t = 2 * h + b
+                    nc.tensor.transpose(
+                        bank[:, kind, b, :], col[:, t : t + 1].to_broadcast([P, P]), ident[:]
+                    )
+            spread.append(bank)
+
+        length = sb.tile([P, 4, BLOCK], F32, name="length", align_bytes=64)
+        gap = sb.tile([P, 4, BLOCK], F32, name="gap", align_bytes=64)
+        res = sb.tile([P, 4, BLOCK], F32, name="res", align_bytes=64)
+        for t in range(4):
             nc.vector.tensor_tensor(
-                diff[:, cs],
+                diff[:, t, :],
                 y[:].indirect(entries(pb_t, t * BLOCK, BLOCK)),
-                y_a[h][:, b * BLOCK : (b + 1) * BLOCK],
+                y_a[:, t * BLOCK : (t + 1) * BLOCK],
                 ALU.subtract,
             )
-            sq = sb.tile([P, BLOCK], F32, name=f"sq{t}", align_bytes=64)
-            ln = sb.tile([P, BLOCK], F32, name=f"ln{t}", align_bytes=64)
-            nc.scalar.activation(sq[:], diff[:, cs], ACT.Square)
-            nc.scalar.activation(ln[:], sq[:], ACT.Sqrt, bias=SOFT)
-            length.append(ln)
+            nc.scalar.activation(sq[:, t, :], diff[:, t, :], ACT.Square)
+            nc.scalar.activation(length[:, t, :], sq[:, t, :], ACT.Sqrt, bias=SOFT)
         for h in range(2):
-            gap = sb.tile([P, HALF], F32, name=f"gap{h}", align_bytes=64)
-            res = sb.tile([P, HALF], F32, name=f"res{h}", align_bytes=64)
             for b in range(2):
                 t = 2 * h + b
-                cs = slice(t * BLOCK, (t + 1) * BLOCK)
-                nc.vector.tensor_tensor(
-                    gap[:, b * BLOCK : (b + 1) * BLOCK], top_rows[:, cs], length[t][:], ALU.subtract
-                )
+                nc.vector.tensor_tensor(gap[:, t, :], spread[h][:, 0, b, :], length[:, t, :], ALU.subtract)
             for b in range(2):
                 t = 2 * h + b
-                cs = slice(t * BLOCK, (t + 1) * BLOCK)
-                bs = slice(b * BLOCK, (b + 1) * BLOCK)
-                nc.vector.tensor_tensor(res[:, bs], gap[:, bs], inv_rows[:, cs], ALU.mult)
-            nc.sync.dma_start(out[:, h * HALF : (h + 1) * HALF], res[:])
+                nc.vector.tensor_tensor(res[:, t, :], gap[:, t, :], spread[h][:, 1, b, :], ALU.mult)
+            nc.sync.dma_start(
+                out[:, h * HALF : (h + 1) * HALF],
+                res[:, 2 * h : 2 * h + 2, :].rearrange("p b c -> p (b c)"),
+            )

@@ -47,17 +47,15 @@ def tile_picked_yxpbd_lam_p_kernel(
         scale_table = sb.tile([P, T], U8, name="scale_table", align_bytes=64)
         word_table = sb.tile([P, T], U32, name="word_table", align_bytes=64)
         im_table = sb.tile([P, S], F32, name="im_table", align_bytes=64)
-        comp_rows = sb.tile([P, U], F32, name="comp_rows", align_bytes=64)
-        w_raw = sb.tile([P, PACK, N], F32, name="w_raw", align_bytes=64)
-        rows = sb.tile([P, BLOCK], F32, name="rows", align_bytes=64)
+        w_raw = shared.tile([P, PACK, N], F32, name="w_raw", align_bytes=64, offset=0)
+        rows = sb.tile([P, U], F32, name="rows", align_bytes=64)
         ident = sb.tile([P, P], F32, name="ident", align_bytes=64)
         one = sb.tile([P, 1], F32, name="one")
         warm = sb.tile([P, 1], F32, name="warm")
 
         nc.vector.memset(scale_table[:].bitcast(I32), 0)
         nc.sync.dma_start(pa_t[:], pa)
-        nc.sync.dma_start(im_table[0:64, :], im[0:64, :])
-        nc.sync.dma_start(comp_rows[0:32, :], comp[0:32, :])
+        nc.sync.dma_start(im_table[0:32, :], im[0:32, :])
         nc.sync.dma_start(offs_t[:], offs)
         nc.sync.dma_start(
             word_table[:].bitcast(I32), x_words[0].rearrange("p n t -> p (n t)").bitcast(I32)
@@ -69,25 +67,21 @@ def tile_picked_yxpbd_lam_p_kernel(
                 x_scales[0, 4 * q : 4 * q + 4, :].bitcast(I32),
             )
         nc.sync.dma_start(pb_t[:], pb)
+        nc.vector.memset(im_table[32:64, :], 0.0)
         nc.vector.memset(im_table[64:128, :], 0.0)
-        nc.vector.memset(comp_rows[32:64, :], 0.0)
-        nc.vector.memset(comp_rows[64:128, :], 0.0)
         nc.gpsimd.memset(one[:], 1.0)
         nc.scalar.activation(warm[:], one[:], ACT.Sqrt)
         nc.gpsimd.memset(rows[:], 0.0)
         make_identity(nc, ident[:])
-        for g, src in enumerate((lam, rest)):
-            blocks = src.rearrange("a (t c) -> (a t) c", c=BLOCK)
-            nc.sync.dma_start(rows[32 * g : 32 * g + 4, :], blocks[0:4, :])
+        for place, src in ((0, comp), (64, lam), (65, rest)):
+            nc.sync.dma_start(rows[place : place + 1, :], src[0:1, :])
 
         im_a = sb.tile([P, U], F32, name="im_a", align_bytes=64)
         for h in range(2):
             cs = slice(h * HALF, (h + 1) * HALF)
-            nc.vector.tensor_tensor(
-                im_a[:, cs], im_table[:].indirect(entries(pa_t, h * HALF, HALF)), comp_rows[:, cs], ALU.add
-            )
+            nc.vector.tensor_copy(im_a[:, cs], im_table[:].indirect(entries(pa_t, h * HALF, HALF)))
 
-        w_grouped = shared.tile([P, N, PACK], BF16, name="w_grouped", align_bytes=64, offset=0)
+        w_grouped = sb.tile([P, N, PACK], BF16, name="w_grouped", align_bytes=64)
         w_codes = sb.tile([P, N], U32, name="w_codes", align_bytes=64)
         w_scales = sb.tile([P, N], U8, name="w_scales", align_bytes=64)
         nc.scalar.copy(w_grouped[:], w_raw[:].rearrange("p j m -> p m j"))
@@ -119,16 +113,23 @@ def tile_picked_yxpbd_lam_p_kernel(
             )
             nc.scalar.copy(y[:, first : first + count], acc[:])
 
-        work = sb.tile([P, 8, BLOCK], F32, name="work", align_bytes=64)
-        diff = work[:, 0:4, :]
-        sq = work[:, 4:8, :]
-        cols = work[:, 2:6, 0:2]
-        rows_t = psum.tile([P, 4, 32], F32, name="rows_t")
-        nc.tensor.transpose(rows_t[:].rearrange("p g c -> p (g c)"), rows[:], ident[:])
-        nc.scalar.copy(cols, rows_t[:, 0:2, 0:4].rearrange("p g t -> p t g"))
+        work = sb.tile([P, 2 * U], F32, name="work", align_bytes=64)
+        blocks_of_work = work[:].rearrange("p (t c) -> p t c", c=BLOCK)
+        diff = blocks_of_work[:, 0:4, :]
+        sq = blocks_of_work[:, 4:8, :]
+        cols = blocks_of_work[:, 1:5, 0:4]
 
         im_sum = shared.tile([P, U], F32, name="im_sum", align_bytes=64, offset=HALF)
-        sum_t = psum.tile([P, 4, 4, 32], F32, name="sum_t")
+        turned = psum.tile([P, 4, BLOCK], F32, name="turned")
+        for t in range(4):
+            nc.tensor.matmul(
+                turned[:, t, :],
+                rows[:, t * BLOCK : (t + 1) * BLOCK],
+                ident[:],
+                start=(t == 0),
+                stop=False,
+                is_transpose=True,
+            )
         for first, blocks in SUM_CHUNKS:
             cs = slice(first * BLOCK, (first + blocks) * BLOCK)
             nc.vector.tensor_tensor(
@@ -138,19 +139,28 @@ def tile_picked_yxpbd_lam_p_kernel(
                 ALU.add,
             )
             for t in range(first, first + blocks):
-                nc.tensor.transpose(
-                    sum_t[:, t].rearrange("p q c -> p (q c)"), im_sum[:, t * BLOCK : (t + 1) * BLOCK], ident[:]
+                nc.tensor.matmul(
+                    turned[:, t, :],
+                    im_sum[:, t * BLOCK : (t + 1) * BLOCK],
+                    ident[:],
+                    start=False,
+                    stop=(t == 3),
+                    is_transpose=True,
                 )
-        sums = sb.tile([P, 2, 4], F32, name="sums")
-        nc.scalar.copy(sums[:], sum_t[:, :, 0:2, 0].rearrange("p t q -> p q t"))
+        den = sb.tile([P, 4], F32, name="den")
+        nc.scalar.copy(den[:], turned[:, :, 0])
+        nc.scalar.copy(
+            cols.rearrange("p t (a b) -> p t a b", b=2),
+            turned[:].rearrange("p t (a c) -> p t a c", a=2)[:, :, :, 0:2],
+        )
         top = sb.tile([P, 4], F32, name="top")
         for t in range(4):
             nc.scalar.activation(
                 top[:, t : t + 1],
-                sums[:, 1, t : t + 1],
+                cols[:, t, 1:2],
                 ACT.Identity,
-                bias=cols[:, t, 1:2],
-                scale=cols[:, t, 0:1],
+                bias=cols[:, t, 3:4],
+                scale=cols[:, t, 2:3],
             )
 
         y_a = sb.tile([P, U], F32, name="y_a", align_bytes=64)
@@ -159,7 +169,7 @@ def tile_picked_yxpbd_lam_p_kernel(
                 y_a[:, h * HALF : (h + 1) * HALF], y[:].indirect(entries(pa_t, h * HALF, HALF))
             )
         inv = sb.tile([P, 4], F32, name="inv")
-        nc.vector.reciprocal(inv[:], sums[:, 0, :])
+        nc.vector.reciprocal(inv[:], den[:])
         spread = []
         for h in range(2):
             bank = psum.tile([P, 2, 2, BLOCK], F32, name=f"spread{h}")

from contextlib import ExitStack

import concourse.mybir as mybir
from concourse.masks import make_identity

K, T, S, N, U = 512, 1024, 512, 128, 512
FLOPS = 2 * K * N * S

F32 = mybir.dt.float32
BF16 = mybir.dt.bfloat16
I32 = mybir.dt.int32
U32 = mybir.dt.uint32
U16 = mybir.dt.uint16
U8 = mybir.dt.uint8
FP8X4 = mybir.dt.float8_e4m3fn_x4
ALU = mybir.AluOpType
ACT = mybir.ActivationFunctionType

P = 128
PACK = 4
LIST_ROWS = 16
HALF = U // 2
BLOCK = 128
SOFT = 0.02
SUM_CHUNKS = ((0, 2), (2, 1), (3, 1))
PICK_CHUNKS = ((0, 256), (256, 128), (384, 128))


def entries(offsets, first, count):
    return offsets[:, first // LIST_ROWS : (first + count) // LIST_ROWS]


def tile_picked_yxpbd_lam_p_kernel(
    tc, x_words, x_scales, w1, im, lam, comp, rest, offs, pa, pb, out
):
    nc = tc.nc
    with ExitStack() as ctx:
        lists = ctx.enter_context(tc.tile_pool(name="lists", bufs=1))
        sb = ctx.enter_context(tc.tile_pool(name="sb", bufs=1))
        shared = ctx.enter_context(tc.tile_pool(name="shared", bufs=1))
        psum = ctx.enter_context(tc.psum_pool(name="psum", bufs=1))

        offs_t = lists.tile([P, S // LIST_ROWS], U16, name="offs_t")
        pa_t = lists.tile([P, U // LIST_ROWS], U16, name="pa_t")
        pb_t = lists.tile([P, U // LIST_ROWS], U16, name="pb_t")

        scale_table = sb.tile([P, T], U8, name="scale_table", align_bytes=64)
        word_table = sb.tile([P, T], U32, name="word_table", align_bytes=64)
        im_table = sb.tile([P, S], F32, name="im_table", align_bytes=64)
        w_raw = shared.tile([P, PACK, N], F32, name="w_raw", align_bytes=64, offset=0)
        rows = sb.tile([P, U], F32, name="rows", align_bytes=64)
        ident = sb.tile([P, P], F32, name="ident", align_bytes=64)
        one = sb.tile([P, 1], F32, name="one")
        warm = sb.tile([P, 1], F32, name="warm")

        nc.vector.memset(scale_table[:].bitcast(I32), 0)
        nc.sync.dma_start(pa_t[:], pa)
        nc.sync.dma_start(im_table[0:32, :], im[0:32, :])
        nc.sync.dma_start(offs_t[:], offs)
        nc.sync.dma_start(
            word_table[:].bitcast(I32), x_words[0].rearrange("p n t -> p (n t)").bitcast(I32)
        )
        nc.sync.dma_start(w_raw[:], w1.rearrange("(p j) m -> p j m", j=PACK))
        for q in range(4):
            nc.sync.dma_start(
                scale_table[32 * q : 32 * q + 4, :].bitcast(I32),
                x_scales[0, 4 * q : 4 * q + 4, :].bitcast(I32),
            )
        nc.sync.dma_start(pb_t[:], pb)
        nc.vector.memset(im_table[32:64, :], 0.0)
        nc.vector.memset(im_table[64:128, :], 0.0)
        nc.gpsimd.memset(one[:], 1.0)
        nc.scalar.activation(warm[:], one[:], ACT.Sqrt)
        nc.gpsimd.memset(rows[:], 0.0)
        make_identity(nc, ident[:])
        for place, src in ((0, comp), (64, lam), (65, rest)):
            nc.sync.dma_start(rows[place : place + 1, :], src[0:1, :])

        im_a = sb.tile([P, U], F32, name="im_a", align_bytes=64)
        for h in range(2):
            cs = slice(h * HALF, (h + 1) * HALF)
            nc.vector.tensor_copy(im_a[:, cs], im_table[:].indirect(entries(pa_t, h * HALF, HALF)))

        w_grouped = sb.tile([P, N, PACK], BF16, name="w_grouped", align_bytes=64)
        w_codes = sb.tile([P, N], U32, name="w_codes", align_bytes=64)
        w_scales = sb.tile([P, N], U8, name="w_scales", align_bytes=64)
        nc.scalar.copy(w_grouped[:], w_raw[:].rearrange("p j m -> p m j"))
        nc.vector.quantize_mx(
            out=w_codes[:].bitcast(FP8X4),
            scales=w_scales[:],
            in_=w_grouped[:].rearrange("p m j -> p (m j)"),
        )

        words = sb.tile([P, S], U32, name="words", align_bytes=64)
        nc.vector.tensor_copy(words[:], word_table[:].indirect(offs_t[:]))

        y = sb.tile([P, S], F32, name="y", align_bytes=64)
        for c, (first, count) in enumerate(PICK_CHUNKS):
            if c == 0:
                scales = sb.tile([P, count], U8, name="scales0", align_bytes=64)
            else:
                scales = shared.tile([P, count], U8, name=f"scales{c}", align_bytes=64, offset=first - HALF)
            nc.vector.tensor_copy(scales[:], scale_table[:].indirect(entries(offs_t, first, count)))
            acc = psum.tile([P, count], F32, name=f"acc{c}")
            nc.tensor.matmul_mx(
                out=acc[:],
                lhsT=w_codes[:].bitcast(FP8X4),
                lhsT_scale=w_scales[:],
                rhs=words[:, first : first + count].bitcast(FP8X4),
                rhs_scale=scales[:],
                start=True,
                stop=True,
            )
            nc.scalar.copy(y[:, first : first + count], acc[:])

        work = sb.tile([P, 2 * U], F32, name="work", align_bytes=64)
        blocks_of_work = work[:].rearrange("p (t c) -> p t c", c=BLOCK)
        diff = blocks_of_work[:, 0:4, :]
        sq = blocks_of_work[:, 4:8, :]
        cols = blocks_of_work[:, 1:5, 0:4]

        im_sum = shared.tile([P, U], F32, name="im_sum", align_bytes=64, offset=HALF)
        turned = psum.tile([P, 4, BLOCK], F32, name="turned")
        for t in range(4):
            nc.tensor.matmul(
                turned[:, t, :],
                rows[:, t * BLOCK : (t + 1) * BLOCK],
                ident[:],
                start=(t == 0),
                stop=False,
                is_transpose=True,
            )
        for first, blocks in SUM_CHUNKS:
            cs = slice(first * BLOCK, (first + blocks) * BLOCK)
            nc.vector.tensor_tensor(
                im_sum[:, cs],
                im_table[:].indirect(entries(pb_t, cs.start, blocks * BLOCK)),
                im_a[:, cs],
                ALU.add,
            )
            for t in range(first, first + blocks):
                nc.tensor.matmul(
                    turned[:, t, :],
                    im_sum[:, t * BLOCK : (t + 1) * BLOCK],
                    ident[:],
                    start=False,
                    stop=(t == 3),
                    is_transpose=True,
                )
        den = sb.tile([P, 4], F32, name="den")
        nc.scalar.copy(den[:], turned[:, :, 0])
        nc.scalar.copy(
            cols.rearrange("p t (a b) -> p t a b", b=2),
            turned[:].rearrange("p t (a c) -> p t a c", a=2)[:, :, :, 0:2],
        )
        top = sb.tile([P, 4], F32, name="top")
        for t in range(4):
            nc.scalar.activation(
                top[:, t : t + 1],
                cols[:, t, 1:2],
                ACT.Identity,
                bias=cols[:, t, 3:4],
                scale=cols[:, t, 2:3],
            )

        y_a = sb.tile([P, U], F32, name="y_a", align_bytes=64)
        for h in range(2):
            nc.vector.tensor_copy(
                y_a[:, h * HALF : (h + 1) * HALF], y[:].indirect(entries(pa_t, h * HALF, HALF))
            )
        inv = sb.tile([P, 4], F32, name="inv")
        nc.vector.reciprocal(inv[:], den[:])
        spread = []
        for h in range(2):
            bank = psum.tile([P, 2, 2, BLOCK], F32, name=f"spread{h}")
            for kind, col in enumerate((top, inv)):
                for b in range(2):
                    t = 2 * h + b
                    nc.tensor.transpose(
                        bank[:, kind, b, :], col[:, t : t + 1].to_broadcast([P, P]), ident[:]
                    )
            spread.append(bank)

        length = sb.tile([P, 4, BLOCK], F32, name="length", align_bytes=64)
        gap = sb.tile([P, 4, BLOCK], F32, name="gap", align_bytes=64)
        res = sb.tile([P, 4, BLOCK], F32, name="res", align_bytes=64)
        for t in range(4):
            nc.vector.tensor_tensor(
                diff[:, t, :],
                y[:].indirect(entries(pb_t, t * BLOCK, BLOCK)),
                y_a[:, t * BLOCK : (t + 1) * BLOCK],
                ALU.subtract,
            )
            nc.scalar.activation(sq[:, t, :], diff[:, t, :], ACT.Square)
            nc.scalar.activation(length[:, t, :], sq[:, t, :], ACT.Sqrt, bias=SOFT)
        for h in range(2):
            for b in range(2):
                t = 2 * h + b
                nc.vector.tensor_tensor(gap[:, t, :], spread[h][:, 0, b, :], length[:, t, :], ALU.subtract)
            for b in range(2):
                t = 2 * h + b
                nc.vector.tensor_tensor(res[:, t, :], gap[:, t, :], spread[h][:, 1, b, :], ALU.mult)
            nc.sync.dma_start(
                out[:, h * HALF : (h + 1) * HALF],
                res[:, 2 * h : 2 * h + 2, :].rearrange("p b c -> p (b c)"),
            )
